import numpy as np
import ml_dtypes


def mxq(x, axis, fmt="e4m3"):
    dtype, down = {"e4m3": (ml_dtypes.float8_e4m3fn, 7), "e5m2": (ml_dtypes.float8_e5m2, 14)}[fmt]
    v = np.moveaxis(np.asarray(x, np.float32).astype(ml_dtypes.bfloat16).astype(np.float64), axis, -1)
    blocks = v.reshape(v.shape[:-1] + (-1, 32))
    amax = np.abs(blocks).max(-1, keepdims=True)
    byte = np.maximum(np.where(amax > 0, np.frexp(amax)[1] - 1 + 127, 0) - down, 1)
    scale = np.exp2(byte - 127.0)
    codes = (blocks / scale).astype(np.float32).astype(dtype).astype(np.float64)
    return np.moveaxis((codes * scale).reshape(v.shape), -1, axis)


WIDE = False


def mx_kscale(k):
    if not WIDE:
        return np.ones(k)
    levels = np.array([10, -10, 5, -5, 0])
    if k % 512:
        return np.exp2(np.random.permutation(np.resize(levels, k // 32))).repeat(32)
    a = np.empty((k // 512, 16))
    for p in range(k // 512):
        a[p, :8] = np.random.permutation(np.resize(levels, 8))
        for g in range(8):
            far = levels[np.abs(levels - a[p, g]) >= 10]
            a[p, g + 8] = far[np.random.randint(len(far))]
    return np.exp2(a.ravel()).repeat(32)


BF16 = ml_dtypes.bfloat16


def bf(x):
    return np.asarray(x, np.float32).astype(BF16)


def f64(x):
    return np.asarray(x).astype(np.float64)


E2M1 = np.array([0.0, 0.5, 1.0, 1.5, 2.0, 3.0, 4.0, 6.0, -0.0, -0.5, -1.0, -1.5, -2.0, -3.0, -4.0, -6.0])


def pack_weight(w, fmt):
    k, n = w.shape
    w = f64(bf(w)).reshape(k // 32, 32, n)
    amax = np.abs(w).max(1)
    if fmt == "e4m3":
        byte = np.frexp(amax)[1] - 1 + 127 - 7
    else:
        mant, ex = np.frexp(amax / 6.0)
        byte = np.where(mant > 0.5, ex, ex - 1) + 127
    byte = np.clip(np.where(amax > 0, byte, 1), 1, 254)
    scaled = (w * np.exp2(127.0 - byte)[:, None, :]).reshape(k, n).astype(np.float32)
    by_word = np.ascontiguousarray(scaled.reshape(k // 512, 128, 4, n).transpose(0, 1, 3, 2))
    if fmt == "e4m3":
        words = by_word.astype(ml_dtypes.float8_e4m3fn).view(np.uint8)
    else:
        c = by_word.astype(ml_dtypes.float4_e2m1fn).view(np.uint8) & 0xF
        words = c[..., 0::2] | (c[..., 1::2] << 4)
    return np.ascontiguousarray(words), np.ascontiguousarray(byte.astype(np.uint8).reshape(k // 512, 16, n))


def unpack_weight(words, scales, fmt):
    g, p, n, _ = words.shape
    if fmt == "e4m3":
        vals = np.ascontiguousarray(words).view(ml_dtypes.float8_e4m3fn).astype(np.float64)
    else:
        nib = np.empty((g, p, n, 4), np.uint8)
        nib[..., 0::2] = words & 0xF
        nib[..., 1::2] = words >> 4
        vals = E2M1[nib]
    vals = vals * np.repeat(np.exp2(scales.astype(np.float64) - 127.0), 8, axis=1)[..., None]
    return vals.transpose(0, 1, 3, 2).reshape(g * 512, n)
def pack4(w):
    words, scales = pack_weight(w, "e2m1")
    return words.reshape(words.shape[0], 128, -1), scales


def unpack4(words, scales):
    return unpack_weight(words.reshape(words.shape[0], 128, -1, 2), scales, "e2m1")


M, K, H, F, D = 1024, 1024, 2, 1024, 512
DELTA = 0.125


def sigmoid(a):
    return 1.0 / (1.0 + np.exp(-a))


def setup_inputs():
    s = mx_kscale(K)
    t = mx_kscale(H * F)
    xw, xs = pack4(np.random.standard_normal((K, M)) * s[:, None])
    uw, us = pack4(np.random.standard_normal((K, H * F)) / np.sqrt(K) / s[:, None])
    gw, gs = pack4(np.random.standard_normal((K, H * D)) / np.sqrt(K) / s[:, None])
    mw, ms = pack4(np.random.standard_normal((H * F, D)) / np.sqrt(F) / t[:, None])
    return {"x_words": xw, "x_scales": xs,
            "wu_words": uw, "wu_scales": us,
            "wg_words": gw, "wg_scales": gs,
            "mem_words": mw, "mem_scales": ms,
            "ubias": bf(0.3 * np.random.standard_normal(H * F)),
            "fscale": bf((1.0 + 0.1 * np.random.standard_normal(H * F)) * t),
            "znorm": bf((0.5 + np.random.random(H * F)) / F / t),
            "gbias": bf(0.3 * np.random.standard_normal(H * D)),
            "local": bf(np.random.standard_normal((M, H * D)))}


def reference(x_words, x_scales, wu_words, wu_scales, wg_words, wg_scales, mem_words, mem_scales,
              ubias, fscale, znorm, gbias, local):
    x = unpack4(x_words, x_scales)
    wu = unpack4(wu_words, wu_scales)
    wg = unpack4(wg_words, wg_scales)
    mem = unpack4(mem_words, mem_scales)
    u = (x.T @ wu) + f64(ubias)
    f = f64(fscale) * np.square(np.maximum(u, 0.0))
    a = sigmoid((x.T @ wg) + f64(gbias))
    z = f64(znorm)
    heads = []
    for j in range(H):
        fj = f[:, j * F:(j + 1) * F]
        num = mxq(fj, 1, "e4m3") @ mem[j * F:(j + 1) * F]
        den = np.sum(fj * z[j * F:(j + 1) * F], axis=1, keepdims=True) + DELTA
        heads.append(num / den)
    att = np.concatenate(heads, axis=1)
    return a * att + (1.0 - a) * f64(local)

@@ -1,0 +1,351 @@
+from contextlib import ExitStack
+
+import concourse.mybir as mybir
+from concourse.masks import make_identity
+
+F32 = mybir.dt.float32
+BF16 = mybir.dt.bfloat16
+I32 = mybir.dt.int32
+U32 = mybir.dt.uint32
+U8 = mybir.dt.uint8
+FP8X4 = mybir.dt.float8_e4m3fn_x4
+FP4X4 = mybir.dt.float4_e2m1fn_x4
+ACT = mybir.ActivationFunctionType
+ALU = mybir.AluOpType
+
+M, K, H, F, D = 1024, 1024, 2, 1024, 512
+DELTA = 0.125
+FLOPS = 2 * M * K * (H * F) + 2 * M * K * (H * D) + 2 * M * H * F * D
+
+P = 128
+T = 4
+KG = K // 512
+NH = 512
+
+
+def tile_relu_squared_memory_read_f2_kernel(
+    tc, x_words, x_scales, wu_words, wu_scales, wg_words, wg_scales, mem_words, mem_scales,
+    ubias, fscale, znorm, gbias, local, out,
+):
+    nc = tc.nc
+    with ExitStack() as ctx:
+        keep = ctx.enter_context(tc.tile_pool(name="keep", bufs=1))
+        work = ctx.enter_context(tc.tile_pool(name="work", bufs=3))
+        psum = ctx.enter_context(tc.psum_pool(name="psum", bufs=1))
+
+        x_w = keep.tile([P, KG, 2 * M], U8, name="x_w", align_bytes=64)
+        x_s = keep.tile([P, KG, M], U8, name="x_s", align_bytes=64)
+        wu_raw = [keep.tile([P, KG, 1024], U8, name="wu_raw%d" % g, align_bytes=64) for g in range(4)]
+        wu_w = [keep.tile([P, KG, 1024], U8, name="wu_w%d" % g, align_bytes=64) for g in range(4)]
+        wus_raw = keep.tile([P, KG, H * F], U8, name="wus_raw", align_bytes=64)
+        wu_s = [keep.tile([P, KG, 512], U8, name="wu_s%d" % g, align_bytes=64) for g in range(4)]
+        wg_w = keep.tile([P, KG, 2 * H * D], U8, name="wg_w", align_bytes=64)
+        wg_s = keep.tile([P, KG, H * D], U8, name="wg_s", align_bytes=64)
+        mem_w = keep.tile([P, 4, 2 * D], U8, name="mem_w", align_bytes=64)
+        mem_s = keep.tile([P, 4, D], U8, name="mem_s", align_bytes=64)
+        loc = [keep.tile([P, 4, 512], BF16, name="loc%d" % s, align_bytes=64) for s in range(4)]
+
+        warm = keep.tile([P, 1], F32, name="warm")
+        nc.vector.memset(warm[:], 0.0)
+        nc.scalar.activation(warm[:], warm[:], ACT.Sigmoid)
+
+        nc.vector.memset(x_s[:].rearrange("p g n -> p (g n)").bitcast(I32), 0)
+        nc.vector.memset(wus_raw[:].rearrange("p g n -> p (g n)").bitcast(I32), 0)
+        nc.gpsimd.memset(wg_s[:].rearrange("p g n -> p (g n)").bitcast(I32), 0)
+        nc.gpsimd.memset(mem_s[:].rearrange("p g n -> p (g n)").bitcast(I32), 0)
+
+        def load_words(dst, src, lo, hi):
+            nc.sync.dma_start(
+                out=dst.bitcast(I32),
+                in_=src[:, :, lo:hi].rearrange("g p c -> p g c").bitcast(I32),
+            )
+
+        def load_scales(plane, src, eng, lo, hi):
+            for q in range(4):
+                eng.dma_start(
+                    out=plane[32 * q : 32 * q + 4, :, lo:hi].bitcast(I32),
+                    in_=src[:, 4 * q : 4 * q + 4, lo:hi].rearrange("g r n -> r g n").bitcast(I32),
+                )
+
+        vec16 = keep.tile([P, 3, 4, T], BF16, name="vec16")
+        for a, v in enumerate((ubias, fscale, znorm)):
+            nc.gpsimd.dma_start(out=vec16[:, a, :, :], in_=v.rearrange("(g p t) -> p g t", p=P, t=T))
+        gb_rows = keep.tile([P, P], BF16, name="gb_rows")
+        nc.gpsimd.memset(gb_rows[:], 0.0)
+        nc.gpsimd.dma_start(out=gb_rows[0:8, :], in_=gbias.rearrange("(c p) -> c p", p=P))
+
+        load_words(wu_raw[0][:], wu_words, 0, 1024)
+        load_scales(wus_raw, wu_scales, nc.sync, 0, 1024)
+        load_words(x_w[:, :, 0:1024], x_words, 0, 1024)
+        load_scales(x_s, x_scales, nc.sync, 0, 1024)
+        load_words(wu_raw[1][:], wu_words, 1024, 2048)
+        load_words(wg_w[:, :, 0:1024], wg_words, 0, 1024)
+        load_scales(wg_s, wg_scales, nc.sync, 0, 1024)
+        load_scales(wus_raw, wu_scales, nc.sync, 1024, 2048)
+        load_words(wu_raw[2][:], wu_words, 2048, 3072)
+        load_words(wu_raw[3][:], wu_words, 3072, 4096)
+        load_words(x_w[:, :, 1024:2048], x_words, 1024, 2048)
+        nc.sync.dma_start(
+            out=mem_w[:].bitcast(I32), in_=mem_words.rearrange("g p c -> p g c").bitcast(I32)
+        )
+        load_scales(mem_s, mem_scales, nc.sync, 0, 512)
+        load_words(wg_w[:, :, 1024:2048], wg_words, 1024, 2048)
+        for s in range(4):
+            j, h = divmod(s, 2)
+            nc.sync.dma_start(
+                out=loc[s][:],
+                in_=local[512 * h : 512 * h + 512, 512 * j : 512 * j + 512].rearrange("(a p) c -> p a c", p=P),
+            )
+
+        ident16 = keep.tile([P, P], BF16, name="ident16")
+        make_identity(nc, ident16[:])
+        ident32 = keep.tile([P, P], F32, name="ident32")
+        make_identity(nc, ident32[:])
+        ones = keep.tile([P, 1], F32, name="ones")
+        nc.vector.memset(ones[:], 1.0)
+
+
+        def permute(g, eng):
+            for kg in range(KG):
+                eng.tensor_copy(
+                    out=wu_w[g][:, kg, :].rearrange("p (t m b) -> p t m b", t=T, b=2),
+                    in_=wu_raw[g][:, kg, :].rearrange("p (m t b) -> p t m b", t=T, b=2),
+                )
+                eng.tensor_copy(
+                    out=wu_s[g][:, kg, :].rearrange("p (t m) -> p t m", t=T),
+                    in_=wus_raw[:, kg, 512 * g : 512 * g + 512].rearrange("p (m t) -> p t m", t=T),
+                )
+
+        gb32 = keep.tile([P, 8], F32, name="gb32")
+        b32 = keep.tile([P, 16], F32, name="b32")
+        fs32 = keep.tile([P, 16], F32, name="fs32")
+        w32 = keep.tile([P, 16], F32, name="w32")
+        vec = vec16[:].rearrange("p a g t -> p a (g t)")
+
+        v_of, q_of, at_of, feat_of, code_of, acc_of, rden_of, fb_of = {}, {}, {}, {}, {}, {}, {}, {}
+        den_of, tp_of, num_of, d_of = {}, {}, {}, {}
+        DIRECT = {i: () for i in range(7)} | {7: (0, 1, 2, 3)}
+        SCALED = (3, 5, 6, 7)
+
+        def where(i):
+            s, gg = divmod(i, 2)
+            j, h = divmod(s, 2)
+            return s, j, h, gg, 2 * j + gg
+
+        def mm_bank(lhs_w, lhs_s, lo, h):
+            bank = psum.tile([P, NH], F32, name="mm", tag="mm", bufs=3)
+            for kg in range(KG):
+                nc.tensor.matmul_mx(
+                    out=bank[:],
+                    lhsT=lhs_w[:, kg, 2 * lo : 2 * lo + 256].bitcast(FP4X4),
+                    lhsT_scale=lhs_s[:, kg, lo : lo + 128],
+                    rhs=x_w[:, kg, 1024 * h : 1024 * h + 1024].bitcast(FP4X4),
+                    rhs_scale=x_s[:, kg, 512 * h : 512 * h + 512],
+                    start=(kg == 0),
+                    stop=(kg == KG - 1),
+                )
+            return bank
+
+        def stage1(i, t):
+            s, j, h, gg, g = where(i)
+            if t == 0:
+                v_of[i] = work.tile([P, T, NH], F32, name="v", tag="v", bufs=2)
+            bank = mm_bank(wu_w[g], wu_s[g], 128 * t, h)
+            nc.scalar.activation(v_of[i][:, t, :], bank[:], ACT.Relu, bias=b32[:, 4 * g + t : 4 * g + t + 1])
+
+        def gate(s, c):
+            j, h = divmod(s, 2)
+            if c == 0:
+                at_of[s] = work.tile([P, 4, NH], F32, name="at", tag="at", bufs=3)
+            bank = mm_bank(wg_w, wg_s, 512 * j + 128 * c, h)
+            nc.scalar.activation(
+                at_of[s][:, c, :], bank[:], ACT.Sigmoid, bias=gb32[:, 4 * j + c : 4 * j + c + 1]
+            )
+
+        def square(i, ts, lo, hi):
+            if i not in q_of:
+                q_of[i] = work.tile([P, T, NH], F32, name="q", tag="q", bufs=4)
+            nc.scalar.activation(q_of[i][:, ts, lo:hi], v_of[i][:, ts, lo:hi], ACT.Square)
+
+        def scaled(i, lo, hi):
+            s, j, h, gg, g = where(i)
+            if i not in fb_of:
+                fb_of[i] = work.tile([P, T, NH], BF16, name="fb", tag="fb", bufs=2)
+            for t in range(T):
+                nc.scalar.activation(fb_of[i][:, t, lo:hi], q_of[i][:, t, lo:hi], ACT.Copy, scale=fs32[:, 4 * g + t : 4 * g + t + 1])
+
+        def den_acc(i):
+            s, j, h, gg, g = where(i)
+            for t in range(T):
+                if t in DIRECT[i]:
+                    continue
+                w = w32[:, 4 * g + t : 4 * g + t + 1]
+                if s not in acc_of:
+                    acc_of[s] = work.tile([P, NH], F32, name="acc", tag="acc", bufs=2)
+                    nc.vector.tensor_scalar_mul(acc_of[s][:], q_of[i][:, t, :], w)
+                else:
+                    acc = acc_of[s]
+                    nc.vector.scalar_tensor_tensor(
+                        out=acc[:], in0=q_of[i][:, t, :], scalar=w, in1=acc[:], op0=ALU.mult, op1=ALU.add
+                    )
+
+        def features(i, lo, hi):
+            s, j, h, gg, g = where(i)
+            if i not in feat_of:
+                feat_of[i] = work.tile([P, NH, T], BF16, name="feat", tag="feat", bufs=3, align_bytes=64)
+            if i in SCALED:
+                nc.vector.tensor_copy(
+                    out=feat_of[i][:, lo:hi, :].rearrange("p (c n) t -> p c t n", n=4),
+                    in_=fb_of[i][:, :, lo:hi].rearrange("p t (c n) -> p c t n", n=4),
+                )
+                return
+            nc.vector.tensor_tensor(
+                out=feat_of[i][:, lo:hi, :],
+                in0=q_of[i][:, :, lo:hi].rearrange("p t n -> p n t"),
+                in1=fs32[:, 4 * g : 4 * g + 4].unsqueeze(1).to_broadcast([P, hi - lo, T]),
+                op=ALU.mult,
+            )
+
+        def quantize(i, lo, hi):
+            if i not in code_of:
+                codes = work.tile([P, NH], U32, name="codes", tag="codes", bufs=5, align_bytes=64)
+                plane = work.tile([P, NH], U8, name="plane", tag="plane", bufs=5, align_bytes=64)
+                code_of[i] = (codes, plane)
+            codes, plane = code_of[i]
+            nc.vector.quantize_mx(
+                out=codes[:, lo:hi].bitcast(FP8X4), scales=plane[:, lo:hi],
+                in_=feat_of[i][:, lo:hi, :].rearrange("p n t -> p (n t)"),
+            )
+
+        def den(s):
+            j, h = divmod(s, 2)
+            bank = psum.tile([P, 4], F32, name="den", tag="den", bufs=1)
+            den_of[s] = bank
+            for a in range(4):
+                cols = slice(128 * a, 128 * a + 128)
+                parts = [(acc_of[s][:, cols], ones[:])] if s in acc_of else []
+                for gg in range(2):
+                    for t in DIRECT[2 * s + gg]:
+                        k = 4 * (2 * j + gg) + t
+                        parts.append((q_of[2 * s + gg][:, t, cols], w32[:, k : k + 1]))
+                for n, (lhs, rhs) in enumerate(parts):
+                    nc.tensor.matmul(
+                        bank[:, a : a + 1], lhsT=lhs, rhs=rhs, start=(n == 0), stop=(n == len(parts) - 1)
+                    )
+
+        def den_inv(s):
+            dsum = work.tile([P, 4], F32, name="dsum", tag="dsum", bufs=2)
+            nc.vector.tensor_scalar_add(dsum[:], den_of[s][:], DELTA)
+            rden_of[s] = work.tile([P, 4], F32, name="rden", tag="rden", bufs=3)
+            nc.vector.reciprocal(rden_of[s][:], dsum[:])
+
+        def turn(s, a):
+            tp = psum.tile([P, NH], F32, name="tp", tag="tp", bufs=2)
+            tp_of[s, a] = tp
+            for c in range(4):
+                nc.tensor.transpose(
+                    tp[:, 128 * c : 128 * c + 128], at_of[s][:, c, 128 * a : 128 * a + 128], ident32[:]
+                )
+
+        def read(s, a):
+            j, h = divmod(s, 2)
+            num = psum.tile([P, D], F32, name="num", tag="num", bufs=2)
+            num_of[s, a] = num
+            for gg in range(2):
+                codes, plane = code_of[2 * s + gg]
+                nc.tensor.matmul_mx(
+                    out=num[:],
+                    lhsT=codes[:, 128 * a : 128 * a + 128].bitcast(FP8X4),
+                    lhsT_scale=plane[:, 128 * a : 128 * a + 128],
+                    rhs=mem_w[:, 2 * j + gg, :].bitcast(FP4X4),
+                    rhs_scale=mem_s[:, 2 * j + gg, :],
+                    start=(gg == 0),
+                    stop=(gg == 1),
+                )
+
+        def blend_d(s, a):
+            d = work.tile([P, D], F32, name="d", tag="d", bufs=4)
+            d_of[s, a] = d
+            nc.vector.scalar_tensor_tensor(
+                out=d[:], in0=num_of[s, a][:], scalar=rden_of[s][:, a : a + 1], in1=loc[s][:, a, :],
+                op0=ALU.mult, op1=ALU.subtract,
+            )
+
+        def blend_e(s, a, eng):
+            j, h = divmod(s, 2)
+            e = work.tile([P, D], F32, name="e", tag="e", bufs=4)
+            nc.vector.tensor_tensor(out=e[:], in0=d_of[s, a][:], in1=tp_of[s, a][:], op=ALU.mult)
+            o = work.tile([P, D], F32, name="o", tag="o", bufs=4)
+            eng.tensor_tensor(out=o[:], in0=e[:], in1=loc[s][:, a, :], op=ALU.add)
+            row = 512 * h + 128 * a
+            nc.sync.dma_start(out=out[row : row + 128, 512 * j : 512 * j + 512], in_=o[:])
+
+
+        everything = slice(0, T)
+        ctx.enter_context(tc.manual_schedule())
+        nc.vector.tensor_copy(out=b32[:], in_=vec[:, 0, :])
+        permute(0, nc.vector)
+        nc.vector.tensor_copy(out=fs32[:], in_=vec[:, 1, :])
+        nc.vector.tensor_tensor(out=w32[:], in0=vec[:, 1, :], in1=vec[:, 2, :], op=ALU.mult)
+        for i in range(9):
+            ps, pp = divmod(i - 3, 2)
+            pair = (2 * pp, 2 * pp + 1) if i >= 3 else ()
+            if i < 8:
+                for t in range(T):
+                    stage1(i, t)
+                    if i == 0:
+                        square(i, t, 0, NH)
+                if i == 0:
+                    permute(1, nc.vector)
+                    permute(2, nc.gpsimd)
+                    permute(3, nc.gpsimd)
+            if i >= 1:
+                if i == 1:
+                    gbt = psum.tile([P, P], BF16, name="gbt", tag="tp", bufs=2)
+                    nc.tensor.transpose(gbt[:], gb_rows[:], ident16[:])
+                    nc.scalar.copy(gb32[:], gbt[:, 0:8])
+                s, gg = divmod(i - 1, 2)
+                gate(s, 2 * gg)
+                gate(s, 2 * gg + 1)
+            if 1 <= i < 7:
+                square(i, everything, 0, NH)
+                if i in SCALED:
+                    scaled(i, 0, NH)
+            if i == 7:
+                for lo in (0, 256):
+                    square(i, everything, lo, lo + 256)
+                    if i in SCALED:
+                        scaled(i, lo, lo + 256)
+            if i >= 3 and i % 2 == 1:
+                den(ps)
+            for a in pair:
+                turn(ps, a)
+            for a in pair:
+                read(ps, a)
+            if i == 1:
+                den_acc(0)
+            if 1 <= i < 8:
+                features(i - 1, 0, NH)
+            if 2 <= i < 8:
+                den_acc(i - 1)
+            if i >= 3 and i % 2 == 1:
+                den_inv(ps)
+            for a in pair:
+                blend_d(ps, a)
+            if 1 <= i < 8:
+                quantize(i - 1, 0, NH)
+            for a in pair:
+                blend_e(ps, a, nc.gpsimd)
+        den(3)
+        for lo in (0, 256):
+            features(7, lo, lo + 256)
+            quantize(7, lo, lo + 256)
+        den_inv(3)
+        for a in range(4):
+            turn(3, a)
+            read(3, a)
+        for a in (0, 2):
+            blend_d(3, a)
+            blend_d(3, a + 1)
+            blend_e(3, a, nc.gpsimd)
+            blend_e(3, a + 1, nc.vector)

@@ -123,9 +123,9 @@ def tile_relu_squared_memory_read_f2_kernel(
         vec = vec16[:].rearrange("p a g t -> p a (g t)")
 
         v_of, q_of, at_of, feat_of, code_of, acc_of, rden_of, fb_of = {}, {}, {}, {}, {}, {}, {}, {}
-        den_of, tp_of, num_of, d_of = {}, {}, {}, {}
+        den_of, tp_of, num_of, d_of, e_of = {}, {}, {}, {}, {}
         DIRECT = {i: () for i in range(7)} | {7: (0, 1, 2, 3)}
-        SCALED = (3, 5, 6, 7)
+        SCALED = (3, 4, 5, 6, 7)
 
         def where(i):
             s, gg = divmod(i, 2)
@@ -200,9 +200,9 @@ def tile_relu_squared_memory_read_f2_kernel(
                 )
                 return
             nc.vector.tensor_tensor(
-                out=feat_of[i][:, lo:hi, :],
-                in0=q_of[i][:, :, lo:hi].rearrange("p t n -> p n t"),
-                in1=fs32[:, 4 * g : 4 * g + 4].unsqueeze(1).to_broadcast([P, hi - lo, T]),
+                out=feat_of[i][:, lo:hi, :].rearrange("p (c n) t -> p c t n", n=4),
+                in0=q_of[i][:, :, lo:hi].rearrange("p t (c n) -> p c t n", n=4),
+                in1=fs32[:, 4 * g : 4 * g + 4].unsqueeze(1).unsqueeze(3).to_broadcast([P, (hi - lo) // 4, T, 4]),
                 op=ALU.mult,
             )
 
@@ -271,10 +271,14 @@ def tile_relu_squared_memory_read_f2_kernel(
                 op0=ALU.mult, op1=ALU.subtract,
             )
 
-        def blend_e(s, a, eng):
-            j, h = divmod(s, 2)
+        def blend_e(s, a):
             e = work.tile([P, D], F32, name="e", tag="e", bufs=4)
             nc.vector.tensor_tensor(out=e[:], in0=d_of[s, a][:], in1=tp_of[s, a][:], op=ALU.mult)
+            e_of[s, a] = e
+
+        def blend_o(s, a, eng):
+            j, h = divmod(s, 2)
+            e = e_of[s, a]
             o = work.tile([P, D], F32, name="o", tag="o", bufs=4)
             eng.tensor_tensor(out=o[:], in0=e[:], in1=loc[s][:, a, :], op=ALU.add)
             row = 512 * h + 128 * a
@@ -297,8 +301,8 @@ def tile_relu_squared_memory_read_f2_kernel(
                         square(i, t, 0, NH)
                 if i == 0:
                     permute(1, nc.vector)
-                    permute(2, nc.gpsimd)
-                    permute(3, nc.gpsimd)
+                    permute(2, nc.vector)
+                    permute(3, nc.vector)
             if i >= 1:
                 if i == 1:
                     gbt = psum.tile([P, P], BF16, name="gbt", tag="tp", bufs=2)
@@ -335,17 +339,21 @@ def tile_relu_squared_memory_read_f2_kernel(
             if 1 <= i < 8:
                 quantize(i - 1, 0, NH)
             for a in pair:
-                blend_e(ps, a, nc.gpsimd)
+                blend_e(ps, a)
+            for a in pair:
+                blend_o(ps, a, nc.vector)
         den(3)
         for lo in (0, 256):
             features(7, lo, lo + 256)
             quantize(7, lo, lo + 256)
         den_inv(3)
-        for a in range(4):
-            turn(3, a)
-            read(3, a)
-        for a in (0, 2):
-            blend_d(3, a)
-            blend_d(3, a + 1)
-            blend_e(3, a, nc.gpsimd)
-            blend_e(3, a + 1, nc.vector)
+        for b in (0, 2):
+            for a in (b, b + 1):
+                turn(3, a)
+                read(3, a)
+            for a in (b, b + 1):
+                blend_d(3, a)
+            for a in (b, b + 1):
+                blend_e(3, a)
+            blend_o(3, b, nc.vector)
+            blend_o(3, b + 1, nc.vector)

from contextlib import ExitStack

import concourse.mybir as mybir
from concourse.masks import make_identity

F32 = mybir.dt.float32
BF16 = mybir.dt.bfloat16
I32 = mybir.dt.int32
U32 = mybir.dt.uint32
U8 = mybir.dt.uint8
FP8X4 = mybir.dt.float8_e4m3fn_x4
FP4X4 = mybir.dt.float4_e2m1fn_x4
ACT = mybir.ActivationFunctionType
ALU = mybir.AluOpType

M, K, H, F, D = 1024, 1024, 2, 1024, 512
DELTA = 0.125
FLOPS = 2 * M * K * (H * F) + 2 * M * K * (H * D) + 2 * M * H * F * D

P = 128
T = 4
KG = K // 512
NH = 512


def tile_relu_squared_memory_read_f2_kernel(
    tc, x_words, x_scales, wu_words, wu_scales, wg_words, wg_scales, mem_words, mem_scales,
    ubias, fscale, znorm, gbias, local, out,
):
    nc = tc.nc
    with ExitStack() as ctx:
        keep = ctx.enter_context(tc.tile_pool(name="keep", bufs=1))
        work = ctx.enter_context(tc.tile_pool(name="work", bufs=3))
        psum = ctx.enter_context(tc.psum_pool(name="psum", bufs=1))

        x_w = keep.tile([P, KG, 2 * M], U8, name="x_w", align_bytes=64)
        x_s = keep.tile([P, KG, M], U8, name="x_s", align_bytes=64)
        wu_raw = [keep.tile([P, KG, 1024], U8, name="wu_raw%d" % g, align_bytes=64) for g in range(4)]
        wu_w = [keep.tile([P, KG, 1024], U8, name="wu_w%d" % g, align_bytes=64) for g in range(4)]
        wus_raw = keep.tile([P, KG, H * F], U8, name="wus_raw", align_bytes=64)
        wu_s = [keep.tile([P, KG, 512], U8, name="wu_s%d" % g, align_bytes=64) for g in range(4)]
        wg_w = keep.tile([P, KG, 2 * H * D], U8, name="wg_w", align_bytes=64)
        wg_s = keep.tile([P, KG, H * D], U8, name="wg_s", align_bytes=64)
        mem_w = keep.tile([P, 4, 2 * D], U8, name="mem_w", align_bytes=64)
        mem_s = keep.tile([P, 4, D], U8, name="mem_s", align_bytes=64)
        loc = [keep.tile([P, 4, 512], BF16, name="loc%d" % s, align_bytes=64) for s in range(4)]

        warm = keep.tile([P, 1], F32, name="warm")
        nc.vector.memset(warm[:], 0.0)
        nc.scalar.activation(warm[:], warm[:], ACT.Sigmoid)

        nc.vector.memset(x_s[:].rearrange("p g n -> p (g n)").bitcast(I32), 0)
        nc.vector.memset(wus_raw[:].rearrange("p g n -> p (g n)").bitcast(I32), 0)
        nc.gpsimd.memset(wg_s[:].rearrange("p g n -> p (g n)").bitcast(I32), 0)
        nc.gpsimd.memset(mem_s[:].rearrange("p g n -> p (g n)").bitcast(I32), 0)

        def load_words(dst, src, lo, hi):
            nc.sync.dma_start(
                out=dst.bitcast(I32),
                in_=src[:, :, lo:hi].rearrange("g p c -> p g c").bitcast(I32),
            )

        def load_scales(plane, src, eng, lo, hi):
            for q in range(4):
                eng.dma_start(
                    out=plane[32 * q : 32 * q + 4, :, lo:hi].bitcast(I32),
                    in_=src[:, 4 * q : 4 * q + 4, lo:hi].rearrange("g r n -> r g n").bitcast(I32),
                )

        vec16 = keep.tile([P, 3, 4, T], BF16, name="vec16")
        for a, v in enumerate((ubias, fscale, znorm)):
            nc.gpsimd.dma_start(out=vec16[:, a, :, :], in_=v.rearrange("(g p t) -> p g t", p=P, t=T))
        gb_rows = keep.tile([P, P], BF16, name="gb_rows")
        nc.gpsimd.memset(gb_rows[:], 0.0)
        nc.gpsimd.dma_start(out=gb_rows[0:8, :], in_=gbias.rearrange("(c p) -> c p", p=P))

        load_words(wu_raw[0][:], wu_words, 0, 1024)
        load_scales(wus_raw, wu_scales, nc.sync, 0, 1024)
        load_words(x_w[:, :, 0:1024], x_words, 0, 1024)
        load_scales(x_s, x_scales, nc.sync, 0, 1024)
        load_words(wu_raw[1][:], wu_words, 1024, 2048)
        load_words(wg_w[:, :, 0:1024], wg_words, 0, 1024)
        load_scales(wg_s, wg_scales, nc.sync, 0, 1024)
        load_scales(wus_raw, wu_scales, nc.sync, 1024, 2048)
        load_words(wu_raw[2][:], wu_words, 2048, 3072)
        load_words(wu_raw[3][:], wu_words, 3072, 4096)
        load_words(x_w[:, :, 1024:2048], x_words, 1024, 2048)
        nc.sync.dma_start(
            out=mem_w[:].bitcast(I32), in_=mem_words.rearrange("g p c -> p g c").bitcast(I32)
        )
        load_scales(mem_s, mem_scales, nc.sync, 0, 512)
        load_words(wg_w[:, :, 1024:2048], wg_words, 1024, 2048)
        for s in range(4):
            j, h = divmod(s, 2)
            nc.sync.dma_start(
                out=loc[s][:],
                in_=local[512 * h : 512 * h + 512, 512 * j : 512 * j + 512].rearrange("(a p) c -> p a c", p=P),
            )

        ident16 = keep.tile([P, P], BF16, name="ident16")
        make_identity(nc, ident16[:])
        ident32 = keep.tile([P, P], F32, name="ident32")
        make_identity(nc, ident32[:])
        ones = keep.tile([P, 1], F32, name="ones")
        nc.vector.memset(ones[:], 1.0)


        def permute(g, eng):
            for kg in range(KG):
                eng.tensor_copy(
                    out=wu_w[g][:, kg, :].rearrange("p (t m b) -> p t m b", t=T, b=2),
                    in_=wu_raw[g][:, kg, :].rearrange("p (m t b) -> p t m b", t=T, b=2),
                )
                eng.tensor_copy(
                    out=wu_s[g][:, kg, :].rearrange("p (t m) -> p t m", t=T),
                    in_=wus_raw[:, kg, 512 * g : 512 * g + 512].rearrange("p (m t) -> p t m", t=T),
                )

        gb32 = keep.tile([P, 8], F32, name="gb32")
        b32 = keep.tile([P, 16], F32, name="b32")
        fs32 = keep.tile([P, 16], F32, name="fs32")
        w32 = keep.tile([P, 16], F32, name="w32")
        vec = vec16[:].rearrange("p a g t -> p a (g t)")

        v_of, q_of, at_of, feat_of, code_of, acc_of, rden_of, fb_of = {}, {}, {}, {}, {}, {}, {}, {}
        den_of, tp_of, num_of, d_of, e_of = {}, {}, {}, {}, {}
        DIRECT = {i: () for i in range(7)} | {7: (0, 1, 2, 3)}
        SCALED = (3, 4, 5, 6, 7)

        def where(i):
            s, gg = divmod(i, 2)
            j, h = divmod(s, 2)
            return s, j, h, gg, 2 * j + gg

        def mm_bank(lhs_w, lhs_s, lo, h):
            bank = psum.tile([P, NH], F32, name="mm", tag="mm", bufs=3)
            for kg in range(KG):
                nc.tensor.matmul_mx(
                    out=bank[:],
                    lhsT=lhs_w[:, kg, 2 * lo : 2 * lo + 256].bitcast(FP4X4),
                    lhsT_scale=lhs_s[:, kg, lo : lo + 128],
                    rhs=x_w[:, kg, 1024 * h : 1024 * h + 1024].bitcast(FP4X4),
                    rhs_scale=x_s[:, kg, 512 * h : 512 * h + 512],
                    start=(kg == 0),
                    stop=(kg == KG - 1),
                )
            return bank

        def stage1(i, t):
            s, j, h, gg, g = where(i)
            if t == 0:
                v_of[i] = work.tile([P, T, NH], F32, name="v", tag="v", bufs=2)
            bank = mm_bank(wu_w[g], wu_s[g], 128 * t, h)
            nc.scalar.activation(v_of[i][:, t, :], bank[:], ACT.Relu, bias=b32[:, 4 * g + t : 4 * g + t + 1])

        def gate(s, c):
            j, h = divmod(s, 2)
            if c == 0:
                at_of[s] = work.tile([P, 4, NH], F32, name="at", tag="at", bufs=3)
            bank = mm_bank(wg_w, wg_s, 512 * j + 128 * c, h)
            nc.scalar.activation(
                at_of[s][:, c, :], bank[:], ACT.Sigmoid, bias=gb32[:, 4 * j + c : 4 * j + c + 1]
            )

        def square(i, ts, lo, hi):
            if i not in q_of:
                q_of[i] = work.tile([P, T, NH], F32, name="q", tag="q", bufs=4)
            nc.scalar.activation(q_of[i][:, ts, lo:hi], v_of[i][:, ts, lo:hi], ACT.Square)

        def scaled(i, lo, hi):
            s, j, h, gg, g = where(i)
            if i not in fb_of:
                fb_of[i] = work.tile([P, T, NH], BF16, name="fb", tag="fb", bufs=2)
            for t in range(T):
                nc.scalar.activation(fb_of[i][:, t, lo:hi], q_of[i][:, t, lo:hi], ACT.Copy, scale=fs32[:, 4 * g + t : 4 * g + t + 1])

        def den_acc(i):
            s, j, h, gg, g = where(i)
            for t in range(T):
                if t in DIRECT[i]:
                    continue
                w = w32[:, 4 * g + t : 4 * g + t + 1]
                if s not in acc_of:
                    acc_of[s] = work.tile([P, NH], F32, name="acc", tag="acc", bufs=2)
                    nc.vector.tensor_scalar_mul(acc_of[s][:], q_of[i][:, t, :], w)
                else:
                    acc = acc_of[s]
                    nc.vector.scalar_tensor_tensor(
                        out=acc[:], in0=q_of[i][:, t, :], scalar=w, in1=acc[:], op0=ALU.mult, op1=ALU.add
                    )

        def features(i, lo, hi):
            s, j, h, gg, g = where(i)
            if i not in feat_of:
                feat_of[i] = work.tile([P, NH, T], BF16, name="feat", tag="feat", bufs=3, align_bytes=64)
            if i in SCALED:
                nc.vector.tensor_copy(
                    out=feat_of[i][:, lo:hi, :].rearrange("p (c n) t -> p c t n", n=4),
                    in_=fb_of[i][:, :, lo:hi].rearrange("p t (c n) -> p c t n", n=4),
                )
                return
            nc.vector.tensor_tensor(
                out=feat_of[i][:, lo:hi, :].rearrange("p (c n) t -> p c t n", n=4),
                in0=q_of[i][:, :, lo:hi].rearrange("p t (c n) -> p c t n", n=4),
                in1=fs32[:, 4 * g : 4 * g + 4].unsqueeze(1).unsqueeze(3).to_broadcast([P, (hi - lo) // 4, T, 4]),
                op=ALU.mult,
            )

        def quantize(i, lo, hi):
            if i not in code_of:
                codes = work.tile([P, NH], U32, name="codes", tag="codes", bufs=5, align_bytes=64)
                plane = work.tile([P, NH], U8, name="plane", tag="plane", bufs=5, align_bytes=64)
                code_of[i] = (codes, plane)
            codes, plane = code_of[i]
            nc.vector.quantize_mx(
                out=codes[:, lo:hi].bitcast(FP8X4), scales=plane[:, lo:hi],
                in_=feat_of[i][:, lo:hi, :].rearrange("p n t -> p (n t)"),
            )

        def den(s):
            j, h = divmod(s, 2)
            bank = psum.tile([P, 4], F32, name="den", tag="den", bufs=1)
            den_of[s] = bank
            for a in range(4):
                cols = slice(128 * a, 128 * a + 128)
                parts = [(acc_of[s][:, cols], ones[:])] if s in acc_of else []
                for gg in range(2):
                    for t in DIRECT[2 * s + gg]:
                        k = 4 * (2 * j + gg) + t
                        parts.append((q_of[2 * s + gg][:, t, cols], w32[:, k : k + 1]))
                for n, (lhs, rhs) in enumerate(parts):
                    nc.tensor.matmul(
                        bank[:, a : a + 1], lhsT=lhs, rhs=rhs, start=(n == 0), stop=(n == len(parts) - 1)
                    )

        def den_inv(s):
            dsum = work.tile([P, 4], F32, name="dsum", tag="dsum", bufs=2)
            nc.vector.tensor_scalar_add(dsum[:], den_of[s][:], DELTA)
            rden_of[s] = work.tile([P, 4], F32, name="rden", tag="rden", bufs=3)
            nc.vector.reciprocal(rden_of[s][:], dsum[:])

        def turn(s, a):
            tp = psum.tile([P, NH], F32, name="tp", tag="tp", bufs=2)
            tp_of[s, a] = tp
            for c in range(4):
                nc.tensor.transpose(
                    tp[:, 128 * c : 128 * c + 128], at_of[s][:, c, 128 * a : 128 * a + 128], ident32[:]
                )

        def read(s, a):
            j, h = divmod(s, 2)
            num = psum.tile([P, D], F32, name="num", tag="num", bufs=2)
            num_of[s, a] = num
            for gg in range(2):
                codes, plane = code_of[2 * s + gg]
                nc.tensor.matmul_mx(
                    out=num[:],
                    lhsT=codes[:, 128 * a : 128 * a + 128].bitcast(FP8X4),
                    lhsT_scale=plane[:, 128 * a : 128 * a + 128],
                    rhs=mem_w[:, 2 * j + gg, :].bitcast(FP4X4),
                    rhs_scale=mem_s[:, 2 * j + gg, :],
                    start=(gg == 0),
                    stop=(gg == 1),
                )

        def blend_d(s, a):
            d = work.tile([P, D], F32, name="d", tag="d", bufs=4)
            d_of[s, a] = d
            nc.vector.scalar_tensor_tensor(
                out=d[:], in0=num_of[s, a][:], scalar=rden_of[s][:, a : a + 1], in1=loc[s][:, a, :],
                op0=ALU.mult, op1=ALU.subtract,
            )

        def blend_e(s, a):
            e = work.tile([P, D], F32, name="e", tag="e", bufs=4)
            nc.vector.tensor_tensor(out=e[:], in0=d_of[s, a][:], in1=tp_of[s, a][:], op=ALU.mult)
            e_of[s, a] = e

        def blend_o(s, a, eng):
            j, h = divmod(s, 2)
            e = e_of[s, a]
            o = work.tile([P, D], F32, name="o", tag="o", bufs=4)
            eng.tensor_tensor(out=o[:], in0=e[:], in1=loc[s][:, a, :], op=ALU.add)
            row = 512 * h + 128 * a
            nc.sync.dma_start(out=out[row : row + 128, 512 * j : 512 * j + 512], in_=o[:])


        everything = slice(0, T)
        ctx.enter_context(tc.manual_schedule())
        nc.vector.tensor_copy(out=b32[:], in_=vec[:, 0, :])
        permute(0, nc.vector)
        nc.vector.tensor_copy(out=fs32[:], in_=vec[:, 1, :])
        nc.vector.tensor_tensor(out=w32[:], in0=vec[:, 1, :], in1=vec[:, 2, :], op=ALU.mult)
        for i in range(9):
            ps, pp = divmod(i - 3, 2)
            pair = (2 * pp, 2 * pp + 1) if i >= 3 else ()
            if i < 8:
                for t in range(T):
                    stage1(i, t)
                    if i == 0:
                        square(i, t, 0, NH)
                if i == 0:
                    permute(1, nc.vector)
                    permute(2, nc.vector)
                    permute(3, nc.vector)
            if i >= 1:
                if i == 1:
                    gbt = psum.tile([P, P], BF16, name="gbt", tag="tp", bufs=2)
                    nc.tensor.transpose(gbt[:], gb_rows[:], ident16[:])
                    nc.scalar.copy(gb32[:], gbt[:, 0:8])
                s, gg = divmod(i - 1, 2)
                gate(s, 2 * gg)
                gate(s, 2 * gg + 1)
            if 1 <= i < 7:
                square(i, everything, 0, NH)
                if i in SCALED:
                    scaled(i, 0, NH)
            if i == 7:
                for lo in (0, 256):
                    square(i, everything, lo, lo + 256)
                    if i in SCALED:
                        scaled(i, lo, lo + 256)
            if i >= 3 and i % 2 == 1:
                den(ps)
            for a in pair:
                turn(ps, a)
            for a in pair:
                read(ps, a)
            if i == 1:
                den_acc(0)
            if 1 <= i < 8:
                features(i - 1, 0, NH)
            if 2 <= i < 8:
                den_acc(i - 1)
            if i >= 3 and i % 2 == 1:
                den_inv(ps)
            for a in pair:
                blend_d(ps, a)
            if 1 <= i < 8:
                quantize(i - 1, 0, NH)
            for a in pair:
                blend_e(ps, a)
            for a in pair:
                blend_o(ps, a, nc.vector)
        den(3)
        for lo in (0, 256):
            features(7, lo, lo + 256)
            quantize(7, lo, lo + 256)
        den_inv(3)
        for b in (0, 2):
            for a in (b, b + 1):
                turn(3, a)
                read(3, a)
            for a in (b, b + 1):
                blend_d(3, a)
            for a in (b, b + 1):
                blend_e(3, a)
            blend_o(3, b, nc.vector)
            blend_o(3, b + 1, nc.vector)
